import numpy as np
import ml_dtypes


def mxq(x, axis, fmt="e4m3"):
    dtype, down = {"e4m3": (ml_dtypes.float8_e4m3fn, 7), "e5m2": (ml_dtypes.float8_e5m2, 14)}[fmt]
    v = np.moveaxis(np.asarray(x, np.float32).astype(ml_dtypes.bfloat16).astype(np.float64), axis, -1)
    blocks = v.reshape(v.shape[:-1] + (-1, 32))
    amax = np.abs(blocks).max(-1, keepdims=True)
    byte = np.maximum(np.where(amax > 0, np.frexp(amax)[1] - 1 + 127, 0) - down, 1)
    scale = np.exp2(byte - 127.0)
    codes = (blocks / scale).astype(np.float32).astype(dtype).astype(np.float64)
    return np.moveaxis((codes * scale).reshape(v.shape), -1, axis)


WIDE = False


def mx_kscale(k):
    if not WIDE:
        return np.ones(k)
    levels = np.array([10, -10, 5, -5, 0])
    if k % 512:
        return np.exp2(np.random.permutation(np.resize(levels, k // 32))).repeat(32)
    a = np.empty((k // 512, 16))
    for p in range(k // 512):
        a[p, :8] = np.random.permutation(np.resize(levels, 8))
        for g in range(8):
            far = levels[np.abs(levels - a[p, g]) >= 10]
            a[p, g + 8] = far[np.random.randint(len(far))]
    return np.exp2(a.ravel()).repeat(32)


def f64(x):
    return np.asarray(x).astype(np.float64)


def striped8(idx):
    return np.asarray(idx).reshape(8, -1, 16).transpose(0, 2, 1).reshape(128, -1).astype(np.uint16)


def unstriped8(offs):
    return offs.reshape(8, 16, -1).transpose(0, 2, 1).reshape(8, -1).astype(np.int64)


def pick8(x, idx, run):
    r = np.arange(len(x))
    return x[r[:, None], idx[r % (8 * run) // run]]


E2M1 = np.array([0.0, 0.5, 1.0, 1.5, 2.0, 3.0, 4.0, 6.0, -0.0, -0.5, -1.0, -1.5, -2.0, -3.0, -4.0, -6.0])


def pack_weight(w, fmt):
    k, n = w.shape
    w = f64(np.asarray(w, np.float32).astype(ml_dtypes.bfloat16)).reshape(k // 32, 32, n)
    amax = np.abs(w).max(1)
    if fmt == "e4m3":
        byte = np.frexp(amax)[1] - 1 + 127 - 7
    else:
        mant, ex = np.frexp(amax / 6.0)
        byte = np.where(mant > 0.5, ex, ex - 1) + 127
    byte = np.clip(np.where(amax > 0, byte, 1), 1, 254)
    scaled = (w * np.exp2(127.0 - byte)[:, None, :]).reshape(k, n).astype(np.float32)
    by_word = np.ascontiguousarray(scaled.reshape(k // 512, 128, 4, n).transpose(0, 1, 3, 2))
    if fmt == "e4m3":
        words = by_word.astype(ml_dtypes.float8_e4m3fn).view(np.uint8)
    else:
        c = by_word.astype(ml_dtypes.float4_e2m1fn).view(np.uint8) & 0xF
        words = (c[..., 0::2] | (c[..., 1::2] << 4)).reshape(k // 512, 128, 2 * n)
    return np.ascontiguousarray(words), np.ascontiguousarray(byte.astype(np.uint8).reshape(k // 512, 16, n))


def unpack_weight(words, scales, fmt):
    g, _, n = scales.shape
    words = np.ascontiguousarray(words).reshape(g, 128, n, -1)
    if fmt == "e4m3":
        vals = words.view(ml_dtypes.float8_e4m3fn).astype(np.float64)
    else:
        nib = np.empty((g, 128, n, 4), np.uint8)
        nib[..., 0::2] = words & 0xF
        nib[..., 1::2] = words >> 4
        vals = E2M1[nib]
    vals = vals * np.repeat(np.exp2(scales.astype(np.float64) - 127.0), 8, axis=1)[..., None]
    return vals.transpose(0, 1, 3, 2).reshape(g * 512, n)


D, T, I, Q, E = 512, 1024, 512, 512, 256


def setup_inputs():
    n = np.random.standard_normal
    idx = np.stack([np.random.permutation(T)[:I] for _ in range(8)])
    idx2 = np.stack([np.random.permutation(T)[:I] for _ in range(8)])
    idx3 = np.stack([np.random.permutation(T)[:I] for _ in range(8)])
    idx4 = np.stack([np.random.permutation(T)[:I] for _ in range(8)])
    idx5 = np.stack([np.random.permutation(T)[:I] for _ in range(8)])
    idx6 = np.stack([np.random.permutation(T)[:I] for _ in range(8)])
    fd = mx_kscale(D)
    fq = mx_kscale(Q)
    cachep = pack_weight(n((D, T)) / fd[:, None], "e4m3")
    mixp = pack_weight(n((Q, E)) * 1.0 / np.sqrt(Q) / fq[:, None], "e2m1")
    return {
        "query": (n((D, Q)) * 1.0 / np.sqrt(D) * fd[:, None]).astype(np.float32),
        "cache_words": cachep[0],
        "cache_scales": cachep[1],
        "rowf": (np.random.uniform(0.5, 2.0, (Q, 1)) * fq[:, None]).astype(np.float32),
        "mix_words": mixp[0],
        "mix_scales": mixp[1],
        "offs": striped8(idx),
        "offs2": striped8(idx2),
        "offs3": striped8(idx3),
        "offs4": striped8(idx4),
        "offs5": striped8(idx5),
        "offs6": striped8(idx6),
    }


def reference(query, cache_words, cache_scales, rowf, mix_words, mix_scales, offs, offs2, offs3, offs4, offs5, offs6):
    idx = unstriped8(offs)
    idx2 = unstriped8(offs2)
    idx3 = unstriped8(offs3)
    idx4 = unstriped8(offs4)
    idx5 = unstriped8(offs5)
    idx6 = unstriped8(offs6)
    cacheu = unpack_weight(cache_words, cache_scales, "e4m3")
    mixu = unpack_weight(mix_words, mix_scales, "e2m1")
    queryq = mxq(f64(query), 0, "e4m3")
    a = queryq.T @ cacheu
    f1 = np.zeros((Q, T))
    f1[np.arange(Q)[:, None], idx2[np.arange(Q) % 512 // 64]] = pick8(a, idx, 64)
    f2 = np.zeros((Q, T))
    f2[np.arange(Q)[:, None], idx4[np.arange(Q) % 512 // 64]] = pick8(a, idx3, 64)
    f3 = np.zeros((Q, T))
    f3[np.arange(Q)[:, None], idx[np.arange(Q) % 512 // 64]] = pick8(a, idx5, 64)
    m1 = np.maximum(f1, f2)
    r = m1 - f3
    g = pick8(r, idx6, 64) + pick8(a, idx3, 64)
    gw = g * f64(rowf)
    gwq = mxq(gw, 0, "e4m3")
    y = mixu.T @ gwq
    return y

@@ -1,0 +1,210 @@
+from contextlib import ExitStack
+
+import concourse.mybir as mybir
+
+D, T, I, Q, E = 512, 1024, 512, 512, 256
+FLOPS = 2 * D * Q * T + 2 * Q * E * I
+
+F32 = mybir.dt.float32
+BF16 = mybir.dt.bfloat16
+I32 = mybir.dt.int32
+U32 = mybir.dt.uint32
+U16 = mybir.dt.uint16
+U8 = mybir.dt.uint8
+FP8X4 = mybir.dt.float8_e4m3fn_x4
+FP4X4 = mybir.dt.float4_e2m1fn_x4
+ALU = mybir.AluOpType
+COPY = mybir.ActivationFunctionType.Copy
+
+P = 128
+PACK = 4
+BANK = 512
+HALF = 256
+
+
+def tile_attend_threewrites_one_mixed_kernel(
+    tc, query, cache_words, cache_scales, rowf, mix_words, mix_scales, offs, offs2, offs3, offs4, offs5, offs6, out
+):
+    nc = tc.nc
+    with ExitStack() as ctx:
+        sb = ctx.enter_context(tc.tile_pool(name="sb", bufs=1))
+        ps = ctx.enter_context(tc.psum_pool(name="ps", bufs=1))
+
+        c_stage = sb.tile([PACK, PACK, T // 4], I32, name="c_stage")
+        nc.sync.dma_start(out=c_stage[:], in_=cache_scales[0].bitcast(I32).rearrange("(g r) c -> r g c", r=PACK))
+        q_raw = []
+        q_rows = query.rearrange("(p j) q -> p j q", j=PACK)
+        for h in range(2):
+            raw = sb.tile([P, PACK, HALF], F32, name="q_raw%d" % h)
+            nc.sync.dma_start(out=raw[:], in_=q_rows[:, :, h * HALF : (h + 1) * HALF])
+            q_raw.append(raw)
+        c_src = cache_words[0].rearrange("p n r -> p (n r)").bitcast(I32)
+        c_words = []
+        for b in range(2):
+            words = sb.tile([P, BANK], I32, name="c_words%d" % b, align_bytes=64)
+            nc.sync.dma_start(out=words[:], in_=c_src[:, b * BANK : (b + 1) * BANK])
+            c_words.append(words)
+        lists = []
+        for n, src in enumerate((offs, offs2, offs3, offs4, offs5, offs6)):
+            lst = sb.tile([P, I // 16], U16, name="list%d" % (n + 1))
+            nc.sync.dma_start(out=lst[:], in_=src)
+            lists.append(lst)
+        idx, idx2, idx3, idx4, idx5, idx6 = lists
+        factor = sb.tile([P, PACK], F32, name="factor")
+        nc.sync.dma_start(out=factor[:], in_=rowf.rearrange("(p t) o -> p (t o)", t=PACK))
+        m_words = sb.tile([P, 2 * E], U8, name="m_words", align_bytes=64)
+        nc.sync.dma_start(out=m_words[:].bitcast(I32), in_=mix_words[0].bitcast(I32))
+        m_plane = sb.tile([P, E], U8, name="m_plane", align_bytes=64)
+        nc.vector.memset(m_plane[:].bitcast(I32), 0)
+        for g in range(PACK):
+            nc.sync.dma_start(
+                out=m_plane[32 * g : 32 * g + PACK, :].bitcast(I32),
+                in_=mix_scales[0, PACK * g : PACK * (g + 1), :].bitcast(I32),
+            )
+
+        c_plane = sb.tile([P, T], U8, name="c_plane", align_bytes=64)
+        nc.vector.memset(c_plane[:].bitcast(I32), 0)
+        for g in range(PACK):
+            nc.vector.tensor_copy(out=c_plane[32 * g : 32 * g + PACK, :].bitcast(I32), in_=c_stage[:, g, :])
+
+        q_dealt = sb.tile([P, PACK, P, PACK], BF16, name="q_dealt", align_bytes=64)
+        for h in range(2):
+            m0 = h * (P // 2)
+            (nc.scalar.copy if h == 0 else nc.vector.tensor_copy)(
+                out=q_dealt[:, :, m0 : m0 + P // 2, :].rearrange("p t m j -> p m j t"),
+                in_=q_raw[h][:].rearrange("p j (m t) -> p m j t", t=PACK),
+            )
+        q_codes = sb.tile([P, Q], U32, name="q_codes", align_bytes=64)
+        q_plane = sb.tile([P, Q], U8, name="q_plane", align_bytes=64)
+        q_flat = q_dealt[:].rearrange("p t m j -> p (t m j)")
+        for c0, c1 in ((0, P), (P, Q)):
+            nc.vector.quantize_mx(
+                out=q_codes[:, c0:c1].bitcast(FP8X4), scales=q_plane[:, c0:c1], in_=q_flat[:, PACK * c0 : PACK * c1]
+            )
+
+        windows = []
+        for s in range(2):
+            trio = [sb.tile([P, T], F32, name="f%d_%d" % (w + 1, s)) for w in range(3)]
+            for win in trio:
+                nc.vector.memset(win[:], 0.0)
+            windows.append(trio)
+
+        banks = [ps.tile([P, BANK], F32, name="bank%d" % b) for b in range(8)]
+        scores = [sb.tile([P, T], F32, name="a%d" % t, tag="a%d" % t) for t in range(PACK)]
+        picked = [[sb.tile([P, I], F32, name="pick%d_%d" % (w, t)) for w in range(3)] for t in range(PACK)]
+        gw = sb.tile([P, I, PACK], BF16, name="gw", align_bytes=64)
+
+        for t in range(PACK):
+            for b in range(2):
+                nc.tensor.matmul_mx(
+                    out=banks[2 * t + b][:],
+                    lhsT=q_codes[:, t * P : (t + 1) * P].bitcast(FP8X4),
+                    lhsT_scale=q_plane[:, t * P : (t + 1) * P],
+                    rhs=c_words[b][:].bitcast(FP8X4),
+                    rhs_scale=c_plane[:, b * BANK : (b + 1) * BANK],
+                    start=True,
+                    stop=True,
+                )
+
+        def unload(t):
+            for b in range(2):
+                dst = scores[t][:, b * BANK : (b + 1) * BANK]
+                if t == 0 and b == 1:
+                    nc.scalar.copy(out=dst, in_=banks[2 * t + b][:])
+                else:
+                    nc.vector.tensor_copy(out=dst, in_=banks[2 * t + b][:])
+
+        def look_up(t):
+            for w, lst in enumerate((idx, idx3, idx5)):
+                n = HALF if t == 0 and w == 0 else I
+                for c in range(0, I, n):
+                    nc.vector.tensor_copy(
+                        out=picked[t][w][:, c : c + n], in_=scores[t][:].indirect(lst[:, c // 16 : (c + n) // 16])
+                    )
+
+        def write(t):
+            for w, lst in enumerate((idx2, idx4, idx)):
+                n = HALF if t == 0 and w == 0 else I
+                for c in range(0, I, n):
+                    nc.scalar.activation(
+                        windows[t % 2][w][:].indirect(lst[:, c // 16 : (c + n) // 16]), picked[t][w][:, c : c + n], COPY
+                    )
+
+        r = sb.tile([P, T], F32, name="r", tag="a2")
+        g_t = [sb.tile([P, I], F32, name="g_%d" % s) for s in range(2)]
+
+        def larger(t):
+            f1, f2, f3 = windows[t % 2]
+            nc.vector.tensor_tensor(r[:], f1[:], f2[:], ALU.max)
+
+        def finish(t, parts):
+            s = t % 2
+            nc.vector.tensor_tensor(r[:], r[:], windows[s][2][:], ALU.subtract)
+            n = I // parts
+            for h in range(parts):
+                nc.vector.tensor_tensor(
+                    g_t[s][:, h * n : (h + 1) * n],
+                    r[:].indirect(idx6[:, h * n // 16 : (h + 1) * n // 16]),
+                    picked[t][1][:, h * n : (h + 1) * n],
+                    ALU.add,
+                )
+            for h in range(parts):
+                nc.vector.tensor_scalar(
+                    out=gw[:, h * n : (h + 1) * n, t],
+                    in0=g_t[s][:, h * n : (h + 1) * n],
+                    scalar1=factor[:, t : t + 1],
+                    scalar2=None,
+                    op0=ALU.mult,
+                )
+
+        unload(0)
+        look_up(0)
+        write(0)
+        unload(1)
+        look_up(1)
+        write(1)
+        unload(2)
+        look_up(2)
+        larger(0)
+        finish(0, 1)
+        write(2)
+        unload(3)
+        look_up(3)
+        larger(1)
+        finish(1, 1)
+        write(3)
+        larger(2)
+        finish(2, 1)
+        larger(3)
+        finish(3, 2)
+
+        g_codes = sb.tile([P, I], U32, name="g_codes", align_bytes=64)
+        g_plane = sb.tile([P, I], U8, name="g_plane", align_bytes=64)
+        gw_flat = gw[:].rearrange("p i t -> p (i t)")
+        out_rows = out.rearrange("(u e) i -> e u i", e=P)
+        for h in range(2):
+            cols = slice(h * HALF, (h + 1) * HALF)
+            nc.vector.quantize_mx(
+                out=g_codes[:, cols].bitcast(FP8X4),
+                scales=g_plane[:, cols],
+                in_=gw_flat[:, PACK * h * HALF : PACK * (h + 1) * HALF],
+            )
+        for h in range(2):
+            cols = slice(h * HALF, (h + 1) * HALF)
+            result = sb.tile([P, 2, HALF], F32, name="result%d" % h)
+            for u in range(2):
+                bank = banks[2 * h + u]
+                nc.tensor.matmul_mx(
+                    out=bank[:, 0:HALF],
+                    lhsT=m_words[:, u * 2 * P : (u + 1) * 2 * P].bitcast(FP4X4),
+                    lhsT_scale=m_plane[:, u * P : (u + 1) * P],
+                    rhs=g_codes[:, cols].bitcast(FP8X4),
+                    rhs_scale=g_plane[:, cols],
+                    start=True,
+                    stop=True,
+                )
+                if h == 1 and u == 1:
+                    nc.vector.tensor_copy(out=result[:, u, :], in_=bank[:, 0:HALF])
+                else:
+                    nc.scalar.copy(out=result[:, u, :], in_=bank[:, 0:HALF])
+            nc.sync.dma_start(out=out_rows[:, :, cols], in_=result[:])

@@ -67,52 +67,56 @@ def tile_attend_threewrites_one_mixed_kernel(
         for g in range(PACK):
             nc.vector.tensor_copy(out=c_plane[32 * g : 32 * g + PACK, :].bitcast(I32), in_=c_stage[:, g, :])
 
-        q_dealt = sb.tile([P, PACK, P, PACK], BF16, name="q_dealt", align_bytes=64)
+        q_first = sb.tile([P, P, PACK], BF16, name="q_first", align_bytes=64)
+        q_rest = sb.tile([P, PACK - 1, P, PACK], BF16, name="q_rest", align_bytes=64)
         for h in range(2):
-            m0 = h * (P // 2)
-            (nc.scalar.copy if h == 0 else nc.vector.tensor_copy)(
-                out=q_dealt[:, :, m0 : m0 + P // 2, :].rearrange("p t m j -> p m j t"),
-                in_=q_raw[h][:].rearrange("p j (m t) -> p m j t", t=PACK),
-            )
+            rows = slice(h * (P // 2), (h + 1) * (P // 2))
+            dealt = q_raw[h][:].rearrange("p j (m t) -> p m j t", t=PACK)
+            nc.vector.tensor_copy(out=q_first[:, rows, :], in_=dealt[:, :, :, 0])
+            nc.scalar.copy(out=q_rest[:, :, rows, :].rearrange("p t m j -> p m j t"), in_=dealt[:, :, :, 1:PACK])
         q_codes = sb.tile([P, Q], U32, name="q_codes", align_bytes=64)
         q_plane = sb.tile([P, Q], U8, name="q_plane", align_bytes=64)
-        q_flat = q_dealt[:].rearrange("p t m j -> p (t m j)")
-        for c0, c1 in ((0, P), (P, Q)):
-            nc.vector.quantize_mx(
-                out=q_codes[:, c0:c1].bitcast(FP8X4), scales=q_plane[:, c0:c1], in_=q_flat[:, PACK * c0 : PACK * c1]
-            )
+        nc.vector.quantize_mx(
+            out=q_codes[:, 0:P].bitcast(FP8X4), scales=q_plane[:, 0:P], in_=q_first[:].rearrange("p m j -> p (m j)")
+        )
+        nc.vector.quantize_mx(
+            out=q_codes[:, P:Q].bitcast(FP8X4), scales=q_plane[:, P:Q], in_=q_rest[:].rearrange("p t m j -> p (t m j)")
+        )
 
-        windows = []
-        for s in range(2):
-            trio = [sb.tile([P, T], F32, name="f%d_%d" % (w + 1, s)) for w in range(3)]
-            for win in trio:
-                nc.vector.memset(win[:], 0.0)
-            windows.append(trio)
+        f1 = [sb.tile([P, T], F32, name="f1_%d" % s) for s in range(2)]
+        f2 = sb.tile([P, T], F32, name="f2")
+        f3 = sb.tile([P, T], F32, name="f3")
+        for win in (f1[0], f2, f3):
+            nc.vector.memset(win[:], 0.0)
+        nc.gpsimd.memset(f1[1][:], 0.0)
+        windows = [(f1[s], f2, f3) for s in range(2)]
 
         banks = [ps.tile([P, BANK], F32, name="bank%d" % b) for b in range(8)]
         scores = [sb.tile([P, T], F32, name="a%d" % t, tag="a%d" % t) for t in range(PACK)]
         picked = [[sb.tile([P, I], F32, name="pick%d_%d" % (w, t)) for w in range(3)] for t in range(PACK)]
         gw = sb.tile([P, I, PACK], BF16, name="gw", align_bytes=64)
 
-        for t in range(PACK):
-            for b in range(2):
+        def pieces(t):
+            if t == 0:
+                return [(banks[b], b * HALF, HALF) for b in range(4)]
+            return [(banks[3 - 2 * b], b * BANK, BANK) for b in range(2)]
+
+        def score(t):
+            for bank, c, n in pieces(t):
                 nc.tensor.matmul_mx(
-                    out=banks[2 * t + b][:],
+                    out=bank[:, 0:n],
                     lhsT=q_codes[:, t * P : (t + 1) * P].bitcast(FP8X4),
                     lhsT_scale=q_plane[:, t * P : (t + 1) * P],
-                    rhs=c_words[b][:].bitcast(FP8X4),
-                    rhs_scale=c_plane[:, b * BANK : (b + 1) * BANK],
+                    rhs=c_words[c // BANK][:, c % BANK : c % BANK + n].bitcast(FP8X4),
+                    rhs_scale=c_plane[:, c : c + n],
                     start=True,
                     stop=True,
                 )
 
         def unload(t):
-            for b in range(2):
-                dst = scores[t][:, b * BANK : (b + 1) * BANK]
-                if t == 0 and b == 1:
-                    nc.scalar.copy(out=dst, in_=banks[2 * t + b][:])
-                else:
-                    nc.vector.tensor_copy(out=dst, in_=banks[2 * t + b][:])
+            for b, (bank, c, n) in enumerate(pieces(t)):
+                copy = nc.scalar.copy if t == 0 and b % 2 == 0 else nc.vector.tensor_copy
+                copy(out=scores[t][:, c : c + n], in_=bank[:, 0:n])
 
         def look_up(t):
             for w, lst in enumerate((idx, idx3, idx5)):
@@ -130,81 +134,83 @@ def tile_attend_threewrites_one_mixed_kernel(
                         windows[t % 2][w][:].indirect(lst[:, c // 16 : (c + n) // 16]), picked[t][w][:, c : c + n], COPY
                     )
 
-        r = sb.tile([P, T], F32, name="r", tag="a2")
+        r = sb.tile([P, T], F32, name="r", tag="a1")
         g_t = [sb.tile([P, I], F32, name="g_%d" % s) for s in range(2)]
 
         def larger(t):
-            f1, f2, f3 = windows[t % 2]
-            nc.vector.tensor_tensor(r[:], f1[:], f2[:], ALU.max)
+            nc.vector.tensor_tensor(r[:], f1[t % 2][:], f2[:], ALU.max)
 
-        def finish(t, parts):
+        def scale(t, c, n):
+            nc.vector.tensor_scalar(
+                out=gw[:, c : c + n, t],
+                in0=g_t[t % 2][:, c : c + n],
+                scalar1=factor[:, t : t + 1],
+                scalar2=None,
+                op0=ALU.mult,
+            )
+
+        def finish(t):
             s = t % 2
             nc.vector.tensor_tensor(r[:], r[:], windows[s][2][:], ALU.subtract)
-            n = I // parts
-            for h in range(parts):
+            if t < PACK - 1:
+                nc.vector.tensor_tensor(g_t[s][:], r[:].indirect(idx6[:]), picked[t][1][:], ALU.add)
+                scale(t, 0, I)
+            else:
+                late = sb.tile([P, HALF], F32, name="late")
+                nc.scalar.activation(late[:], r[:].indirect(idx6[:, HALF // 16 :]), COPY)
                 nc.vector.tensor_tensor(
-                    g_t[s][:, h * n : (h + 1) * n],
-                    r[:].indirect(idx6[:, h * n // 16 : (h + 1) * n // 16]),
-                    picked[t][1][:, h * n : (h + 1) * n],
-                    ALU.add,
+                    g_t[s][:, 0:HALF], r[:].indirect(idx6[:, 0 : HALF // 16]), picked[t][1][:, 0:HALF], ALU.add
                 )
-            for h in range(parts):
-                nc.vector.tensor_scalar(
-                    out=gw[:, h * n : (h + 1) * n, t],
-                    in0=g_t[s][:, h * n : (h + 1) * n],
-                    scalar1=factor[:, t : t + 1],
-                    scalar2=None,
-                    op0=ALU.mult,
-                )
+                nc.vector.tensor_tensor(g_t[s][:, HALF:I], late[:], picked[t][1][:, HALF:I], ALU.add)
 
+        score(0)
         unload(0)
         look_up(0)
-        write(0)
-        unload(1)
-        look_up(1)
-        write(1)
-        unload(2)
-        look_up(2)
-        larger(0)
-        finish(0, 1)
-        write(2)
-        unload(3)
-        look_up(3)
-        larger(1)
-        finish(1, 1)
-        write(3)
-        larger(2)
-        finish(2, 1)
-        larger(3)
-        finish(3, 2)
+        for t in range(PACK):
+            write(t)
+            if t + 1 < PACK:
+                if t == 0:
+                    score(1)
+                    unload(1)
+                look_up(t + 1)
+            larger(t)
+            if t + 2 < PACK:
+                score(t + 2)
+                unload(t + 2)
+            finish(t)
 
         g_codes = sb.tile([P, I], U32, name="g_codes", align_bytes=64)
         g_plane = sb.tile([P, I], U8, name="g_plane", align_bytes=64)
         gw_flat = gw[:].rearrange("p i t -> p (i t)")
         out_rows = out.rearrange("(u e) i -> e u i", e=P)
-        for h in range(2):
-            cols = slice(h * HALF, (h + 1) * HALF)
+        parts = ((0, HALF), (HALF, P), (HALF + P, P))
+
+        def quantise(c, n):
             nc.vector.quantize_mx(
-                out=g_codes[:, cols].bitcast(FP8X4),
-                scales=g_plane[:, cols],
-                in_=gw_flat[:, PACK * h * HALF : PACK * (h + 1) * HALF],
+                out=g_codes[:, c : c + n].bitcast(FP8X4),
+                scales=g_plane[:, c : c + n],
+                in_=gw_flat[:, PACK * c : PACK * (c + n)],
             )
-        for h in range(2):
-            cols = slice(h * HALF, (h + 1) * HALF)
-            result = sb.tile([P, 2, HALF], F32, name="result%d" % h)
+
+        scale(PACK - 1, *parts[0])
+        scale(PACK - 1, *parts[1])
+        quantise(*parts[0])
+        scale(PACK - 1, *parts[2])
+        quantise(*parts[1])
+        quantise(*parts[2])
+        for k, (c, n) in enumerate(parts):
+            result = sb.tile([P, 2, n], F32, name="result%d" % k)
             for u in range(2):
-                bank = banks[2 * h + u]
+                bank = banks[2 + 2 * k + u]
                 nc.tensor.matmul_mx(
-                    out=bank[:, 0:HALF],
+                    out=bank[:, 0:n],
                     lhsT=m_words[:, u * 2 * P : (u + 1) * 2 * P].bitcast(FP4X4),
                     lhsT_scale=m_plane[:, u * P : (u + 1) * P],
-                    rhs=g_codes[:, cols].bitcast(FP8X4),
-                    rhs_scale=g_plane[:, cols],
+                    rhs=g_codes[:, c : c + n].bitcast(FP8X4),
+                    rhs_scale=g_plane[:, c : c + n],
                     start=True,
                     stop=True,
                 )
-                if h == 1 and u == 1:
-                    nc.vector.tensor_copy(out=result[:, u, :], in_=bank[:, 0:HALF])
-                else:
-                    nc.scalar.copy(out=result[:, u, :], in_=bank[:, 0:HALF])
-            nc.sync.dma_start(out=out_rows[:, :, cols], in_=result[:])
+                copy = nc.vector.tensor_copy if k == len(parts) - 1 and u == 1 else nc.scalar.copy
+                copy(out=result[:, u, :], in_=bank[:, 0:n])
+            nc.sync.dma_start(out=out_rows[:, :, c : c + n], in_=result[:])

@@ -64,36 +64,31 @@ def tile_attend_threewrites_one_mixed_kernel(
 
         c_plane = sb.tile([P, T], U8, name="c_plane", align_bytes=64)
         nc.vector.memset(c_plane[:].bitcast(I32), 0)
-        for g in range(PACK):
-            nc.vector.tensor_copy(out=c_plane[32 * g : 32 * g + PACK, :].bitcast(I32), in_=c_stage[:, g, :])
-
-        q_first = sb.tile([P, P, PACK], BF16, name="q_first", align_bytes=64)
-        q_rest = sb.tile([P, PACK - 1, P, PACK], BF16, name="q_rest", align_bytes=64)
-        for h in range(2):
-            rows = slice(h * (P // 2), (h + 1) * (P // 2))
-            dealt = q_raw[h][:].rearrange("p j (m t) -> p m j t", t=PACK)
-            nc.vector.tensor_copy(out=q_first[:, rows, :], in_=dealt[:, :, :, 0])
-            nc.scalar.copy(out=q_rest[:, :, rows, :].rearrange("p t m j -> p m j t"), in_=dealt[:, :, :, 1:PACK])
-        q_codes = sb.tile([P, Q], U32, name="q_codes", align_bytes=64)
-        q_plane = sb.tile([P, Q], U8, name="q_plane", align_bytes=64)
-        nc.vector.quantize_mx(
-            out=q_codes[:, 0:P].bitcast(FP8X4), scales=q_plane[:, 0:P], in_=q_first[:].rearrange("p m j -> p (m j)")
-        )
-        nc.vector.quantize_mx(
-            out=q_codes[:, P:Q].bitcast(FP8X4), scales=q_plane[:, P:Q], in_=q_rest[:].rearrange("p t m j -> p (t m j)")
-        )
-
-        f1 = [sb.tile([P, T], F32, name="f1_%d" % s) for s in range(2)]
+        f1 = [sb.tile([P, T], F32, name="f1_0")]
         f2 = sb.tile([P, T], F32, name="f2")
         f3 = sb.tile([P, T], F32, name="f3")
         for win in (f1[0], f2, f3):
             nc.vector.memset(win[:], 0.0)
-        nc.gpsimd.memset(f1[1][:], 0.0)
-        windows = [(f1[s], f2, f3) for s in range(2)]
+        for g in range(PACK):
+            nc.vector.tensor_copy(out=c_plane[32 * g : 32 * g + PACK, :].bitcast(I32), in_=c_stage[:, g, :])
+
+        q_dealt = sb.tile([P, PACK, P, PACK], BF16, name="q_dealt", align_bytes=64)
+        for h in range(2):
+            rows = slice(h * (P // 2), (h + 1) * (P // 2))
+            dealt = q_raw[h][:].rearrange("p j (m t) -> p m j t", t=PACK)
+            for copy, pair in ((nc.vector.tensor_copy, slice(0, 2)), (nc.scalar.copy, slice(2, 4))):
+                copy(out=q_dealt[:, pair, rows, :].rearrange("p t m j -> p m j t"), in_=dealt[:, :, :, pair])
+        q_codes = sb.tile([P, Q], U32, name="q_codes", align_bytes=64)
+        q_plane = sb.tile([P, Q], U8, name="q_plane", align_bytes=64)
+        q_flat = q_dealt[:].rearrange("p t m j -> p (t m j)")
+        for c0, c1 in ((0, P), (P, Q)):
+            nc.vector.quantize_mx(
+                out=q_codes[:, c0:c1].bitcast(FP8X4), scales=q_plane[:, c0:c1], in_=q_flat[:, PACK * c0 : PACK * c1]
+            )
 
         banks = [ps.tile([P, BANK], F32, name="bank%d" % b) for b in range(8)]
         scores = [sb.tile([P, T], F32, name="a%d" % t, tag="a%d" % t) for t in range(PACK)]
-        picked = [[sb.tile([P, I], F32, name="pick%d_%d" % (w, t)) for w in range(3)] for t in range(PACK)]
+        picked = [[sb.tile([P, I], F32, name="pick%d_%d" % (w, t), tag="pick%d_%d" % (w, t)) for w in range(3)] for t in range(PACK)]
         gw = sb.tile([P, I, PACK], BF16, name="gw", align_bytes=64)
 
         def pieces(t):
@@ -118,21 +113,22 @@ def tile_attend_threewrites_one_mixed_kernel(
                 copy = nc.scalar.copy if t == 0 and b % 2 == 0 else nc.vector.tensor_copy
                 copy(out=scores[t][:, c : c + n], in_=bank[:, 0:n])
 
+        def cuts(t):
+            if t == 0:
+                return [(w, c, HALF) for c in (0, HALF) for w in (0, 1)] + [(2, 0, I)]
+            return [(w, 0, I) for w in range(3)]
+
         def look_up(t):
-            for w, lst in enumerate((idx, idx3, idx5)):
-                n = HALF if t == 0 and w == 0 else I
-                for c in range(0, I, n):
-                    nc.vector.tensor_copy(
-                        out=picked[t][w][:, c : c + n], in_=scores[t][:].indirect(lst[:, c // 16 : (c + n) // 16])
-                    )
+            for w, c, n in cuts(t):
+                lst = (idx, idx3, idx5)[w]
+                nc.vector.tensor_copy(
+                    out=picked[t][w][:, c : c + n], in_=scores[t][:].indirect(lst[:, c // 16 : (c + n) // 16])
+                )
 
         def write(t):
-            for w, lst in enumerate((idx2, idx4, idx)):
-                n = HALF if t == 0 and w == 0 else I
-                for c in range(0, I, n):
-                    nc.scalar.activation(
-                        windows[t % 2][w][:].indirect(lst[:, c // 16 : (c + n) // 16]), picked[t][w][:, c : c + n], COPY
-                    )
+            for w, c, n in cuts(t):
+                win, lst = ((f1[t % 2], idx2), (f2, idx4), (f3, idx))[w]
+                nc.scalar.activation(win[:].indirect(lst[:, c // 16 : (c + n) // 16]), picked[t][w][:, c : c + n], COPY)
 
         r = sb.tile([P, T], F32, name="r", tag="a1")
         g_t = [sb.tile([P, I], F32, name="g_%d" % s) for s in range(2)]
@@ -151,7 +147,7 @@ def tile_attend_threewrites_one_mixed_kernel(
 
         def finish(t):
             s = t % 2
-            nc.vector.tensor_tensor(r[:], r[:], windows[s][2][:], ALU.subtract)
+            nc.vector.tensor_tensor(r[:], r[:], f3[:], ALU.subtract)
             if t < PACK - 1:
                 nc.vector.tensor_tensor(g_t[s][:], r[:].indirect(idx6[:]), picked[t][1][:], ALU.add)
                 scale(t, 0, I)
@@ -161,6 +157,7 @@ def tile_attend_threewrites_one_mixed_kernel(
                 nc.vector.tensor_tensor(
                     g_t[s][:, 0:HALF], r[:].indirect(idx6[:, 0 : HALF // 16]), picked[t][1][:, 0:HALF], ALU.add
                 )
+                scale(t, 0, HALF)
                 nc.vector.tensor_tensor(g_t[s][:, HALF:I], late[:], picked[t][1][:, HALF:I], ALU.add)
 
         score(0)
@@ -168,6 +165,9 @@ def tile_attend_threewrites_one_mixed_kernel(
         look_up(0)
         for t in range(PACK):
             write(t)
+            if t == 0:
+                f1.append(sb.tile([P, T], F32, name="f1_1", tag="pick0_0"))
+                nc.gpsimd.memset(f1[1][:], 0.0)
             if t + 1 < PACK:
                 if t == 0:
                     score(1)
@@ -192,9 +192,8 @@ def tile_attend_threewrites_one_mixed_kernel(
                 in_=gw_flat[:, PACK * c : PACK * (c + n)],
             )
 
-        scale(PACK - 1, *parts[0])
-        scale(PACK - 1, *parts[1])
         quantise(*parts[0])
+        scale(PACK - 1, *parts[1])
         scale(PACK - 1, *parts[2])
         quantise(*parts[1])
         quantise(*parts[2])

@@ -28,6 +28,7 @@ def tile_attend_threewrites_one_mixed_kernel(
     nc = tc.nc
     with ExitStack() as ctx:
         sb = ctx.enter_context(tc.tile_pool(name="sb", bufs=1))
+        placed = ctx.enter_context(tc.tile_pool(name="placed", bufs=1))
         ps = ctx.enter_context(tc.psum_pool(name="ps", bufs=1))
 
         c_stage = sb.tile([PACK, PACK, T // 4], I32, name="c_stage")
@@ -39,11 +40,8 @@ def tile_attend_threewrites_one_mixed_kernel(
             nc.sync.dma_start(out=raw[:], in_=q_rows[:, :, h * HALF : (h + 1) * HALF])
             q_raw.append(raw)
         c_src = cache_words[0].rearrange("p n r -> p (n r)").bitcast(I32)
-        c_words = []
-        for b in range(2):
-            words = sb.tile([P, BANK], I32, name="c_words%d" % b, align_bytes=64)
-            nc.sync.dma_start(out=words[:], in_=c_src[:, b * BANK : (b + 1) * BANK])
-            c_words.append(words)
+        c_words = sb.tile([P, T], I32, name="c_words", align_bytes=64)
+        nc.sync.dma_start(out=c_words[:], in_=c_src)
         lists = []
         for n, src in enumerate((offs, offs2, offs3, offs4, offs5, offs6)):
             lst = sb.tile([P, I // 16], U16, name="list%d" % (n + 1))
@@ -56,10 +54,10 @@ def tile_attend_threewrites_one_mixed_kernel(
         nc.sync.dma_start(out=m_words[:].bitcast(I32), in_=mix_words[0].bitcast(I32))
         m_plane = sb.tile([P, E], U8, name="m_plane", align_bytes=64)
         nc.vector.memset(m_plane[:].bitcast(I32), 0)
-        for g in range(PACK):
+        for quad in range(PACK):
             nc.sync.dma_start(
-                out=m_plane[32 * g : 32 * g + PACK, :].bitcast(I32),
-                in_=mix_scales[0, PACK * g : PACK * (g + 1), :].bitcast(I32),
+                out=m_plane[32 * quad : 32 * quad + PACK, :].bitcast(I32),
+                in_=mix_scales[0, PACK * quad : PACK * (quad + 1), :].bitcast(I32),
             )
 
         c_plane = sb.tile([P, T], U8, name="c_plane", align_bytes=64)
@@ -69,8 +67,8 @@ def tile_attend_threewrites_one_mixed_kernel(
         f3 = sb.tile([P, T], F32, name="f3")
         for win in (f1[0], f2, f3):
             nc.vector.memset(win[:], 0.0)
-        for g in range(PACK):
-            nc.vector.tensor_copy(out=c_plane[32 * g : 32 * g + PACK, :].bitcast(I32), in_=c_stage[:, g, :])
+        for quad in range(PACK):
+            nc.vector.tensor_copy(out=c_plane[32 * quad : 32 * quad + PACK, :].bitcast(I32), in_=c_stage[:, quad, :])
 
         q_dealt = sb.tile([P, PACK, P, PACK], BF16, name="q_dealt", align_bytes=64)
         for h in range(2):
@@ -87,7 +85,8 @@ def tile_attend_threewrites_one_mixed_kernel(
             )
 
         banks = [ps.tile([P, BANK], F32, name="bank%d" % b) for b in range(8)]
-        scores = [sb.tile([P, T], F32, name="a%d" % t, tag="a%d" % t) for t in range(PACK)]
+        scores = [sb.tile([P, T], F32, name="a%d" % t, tag="a%d" % t) for t in range(PACK - 1)]
+        scores.append(placed.tile([P, T], F32, name="a3", offset=0))
         picked = [[sb.tile([P, I], F32, name="pick%d_%d" % (w, t), tag="pick%d_%d" % (w, t)) for w in range(3)] for t in range(PACK)]
         gw = sb.tile([P, I, PACK], BF16, name="gw", align_bytes=64)
 
@@ -102,7 +101,7 @@ def tile_attend_threewrites_one_mixed_kernel(
                     out=bank[:, 0:n],
                     lhsT=q_codes[:, t * P : (t + 1) * P].bitcast(FP8X4),
                     lhsT_scale=q_plane[:, t * P : (t + 1) * P],
-                    rhs=c_words[c // BANK][:, c % BANK : c % BANK + n].bitcast(FP8X4),
+                    rhs=c_words[:, c : c + n].bitcast(FP8X4),
                     rhs_scale=c_plane[:, c : c + n],
                     start=True,
                     stop=True,
@@ -130,54 +129,56 @@ def tile_attend_threewrites_one_mixed_kernel(
                 win, lst = ((f1[t % 2], idx2), (f2, idx4), (f3, idx))[w]
                 nc.scalar.activation(win[:].indirect(lst[:, c // 16 : (c + n) // 16]), picked[t][w][:, c : c + n], COPY)
 
-        r = sb.tile([P, T], F32, name="r", tag="a1")
-        g_t = [sb.tile([P, I], F32, name="g_%d" % s) for s in range(2)]
+        r = [sb.tile([P, T], F32, name="r%d" % t, tag="a%d" % (t + 1)) for t in range(2)]
+        r += [placed.tile([P, T], F32, name="r2", offset=4 * I)] * 2
+        g = placed.tile([P, I], F32, name="g", offset=0)
 
         def larger(t):
-            nc.vector.tensor_tensor(r[:], f1[t % 2][:], f2[:], ALU.max)
+            nc.vector.tensor_tensor(r[t][:], f1[t % 2][:], f2[:], ALU.max)
+
+        def less(t):
+            nc.vector.tensor_tensor(r[t][:], r[t][:], f3[:], ALU.subtract)
+
+        def read_back(t, n):
+            nc.vector.tensor_tensor(g[:, 0:n], r[t][:].indirect(idx6[:, 0 : n // 16]), picked[t][1][:, 0:n], ALU.add)
 
         def scale(t, c, n):
             nc.vector.tensor_scalar(
-                out=gw[:, c : c + n, t],
-                in0=g_t[t % 2][:, c : c + n],
-                scalar1=factor[:, t : t + 1],
-                scalar2=None,
-                op0=ALU.mult,
+                out=gw[:, c : c + n, t], in0=g[:, c : c + n], scalar1=factor[:, t : t + 1], scalar2=None, op0=ALU.mult
             )
-
-        def finish(t):
-            s = t % 2
-            nc.vector.tensor_tensor(r[:], r[:], f3[:], ALU.subtract)
-            if t < PACK - 1:
-                nc.vector.tensor_tensor(g_t[s][:], r[:].indirect(idx6[:]), picked[t][1][:], ALU.add)
-                scale(t, 0, I)
-            else:
-                late = sb.tile([P, HALF], F32, name="late")
-                nc.scalar.activation(late[:], r[:].indirect(idx6[:, HALF // 16 :]), COPY)
-                nc.vector.tensor_tensor(
-                    g_t[s][:, 0:HALF], r[:].indirect(idx6[:, 0 : HALF // 16]), picked[t][1][:, 0:HALF], ALU.add
-                )
-                scale(t, 0, HALF)
-                nc.vector.tensor_tensor(g_t[s][:, HALF:I], late[:], picked[t][1][:, HALF:I], ALU.add)
 
         score(0)
         unload(0)
         look_up(0)
-        for t in range(PACK):
-            write(t)
-            if t == 0:
-                f1.append(sb.tile([P, T], F32, name="f1_1", tag="pick0_0"))
-                nc.gpsimd.memset(f1[1][:], 0.0)
-            if t + 1 < PACK:
-                if t == 0:
-                    score(1)
-                    unload(1)
-                look_up(t + 1)
+        write(0)
+        f1.append(sb.tile([P, T], F32, name="f1_1", tag="pick0_0"))
+        nc.gpsimd.memset(f1[1][:], 0.0)
+        score(1)
+        unload(1)
+        look_up(1)
+        for t in range(2):
             larger(t)
-            if t + 2 < PACK:
-                score(t + 2)
-                unload(t + 2)
-            finish(t)
+            score(t + 2)
+            unload(t + 2)
+            less(t)
+            write(t + 1)
+            look_up(t + 2)
+        read_back(0, I)
+        larger(2)
+        scale(0, 0, I)
+        less(2)
+        write(3)
+        read_back(1, I)
+        scale(1, 0, I)
+        read_back(2, I)
+        larger(3)
+        scale(2, 0, I)
+        less(3)
+        late = sb.tile([P, HALF], F32, name="late")
+        nc.scalar.activation(late[:], r[3][:].indirect(idx6[:, HALF // 16 :]), COPY)
+        read_back(3, HALF)
+        scale(3, 0, HALF)
+        nc.vector.tensor_tensor(g[:, HALF:I], late[:], picked[3][1][:, HALF:I], ALU.add)
 
         g_codes = sb.tile([P, I], U32, name="g_codes", align_bytes=64)
         g_plane = sb.tile([P, I], U8, name="g_plane", align_bytes=64)

from contextlib import ExitStack

import concourse.mybir as mybir

D, T, I, Q, E = 512, 1024, 512, 512, 256
FLOPS = 2 * D * Q * T + 2 * Q * E * I

F32 = mybir.dt.float32
BF16 = mybir.dt.bfloat16
I32 = mybir.dt.int32
U32 = mybir.dt.uint32
U16 = mybir.dt.uint16
U8 = mybir.dt.uint8
FP8X4 = mybir.dt.float8_e4m3fn_x4
FP4X4 = mybir.dt.float4_e2m1fn_x4
ALU = mybir.AluOpType
COPY = mybir.ActivationFunctionType.Copy

P = 128
PACK = 4
BANK = 512
HALF = 256


def tile_attend_threewrites_one_mixed_kernel(
    tc, query, cache_words, cache_scales, rowf, mix_words, mix_scales, offs, offs2, offs3, offs4, offs5, offs6, out
):
    nc = tc.nc
    with ExitStack() as ctx:
        sb = ctx.enter_context(tc.tile_pool(name="sb", bufs=1))
        placed = ctx.enter_context(tc.tile_pool(name="placed", bufs=1))
        ps = ctx.enter_context(tc.psum_pool(name="ps", bufs=1))

        c_stage = sb.tile([PACK, PACK, T // 4], I32, name="c_stage")
        nc.sync.dma_start(out=c_stage[:], in_=cache_scales[0].bitcast(I32).rearrange("(g r) c -> r g c", r=PACK))
        q_raw = []
        q_rows = query.rearrange("(p j) q -> p j q", j=PACK)
        for h in range(2):
            raw = sb.tile([P, PACK, HALF], F32, name="q_raw%d" % h)
            nc.sync.dma_start(out=raw[:], in_=q_rows[:, :, h * HALF : (h + 1) * HALF])
            q_raw.append(raw)
        c_src = cache_words[0].rearrange("p n r -> p (n r)").bitcast(I32)
        c_words = sb.tile([P, T], I32, name="c_words", align_bytes=64)
        nc.sync.dma_start(out=c_words[:], in_=c_src)
        lists = []
        for n, src in enumerate((offs, offs2, offs3, offs4, offs5, offs6)):
            lst = sb.tile([P, I // 16], U16, name="list%d" % (n + 1))
            nc.sync.dma_start(out=lst[:], in_=src)
            lists.append(lst)
        idx, idx2, idx3, idx4, idx5, idx6 = lists
        factor = sb.tile([P, PACK], F32, name="factor")
        nc.sync.dma_start(out=factor[:], in_=rowf.rearrange("(p t) o -> p (t o)", t=PACK))
        m_words = sb.tile([P, 2 * E], U8, name="m_words", align_bytes=64)
        nc.sync.dma_start(out=m_words[:].bitcast(I32), in_=mix_words[0].bitcast(I32))
        m_plane = sb.tile([P, E], U8, name="m_plane", align_bytes=64)
        nc.vector.memset(m_plane[:].bitcast(I32), 0)
        for quad in range(PACK):
            nc.sync.dma_start(
                out=m_plane[32 * quad : 32 * quad + PACK, :].bitcast(I32),
                in_=mix_scales[0, PACK * quad : PACK * (quad + 1), :].bitcast(I32),
            )

        c_plane = sb.tile([P, T], U8, name="c_plane", align_bytes=64)
        nc.vector.memset(c_plane[:].bitcast(I32), 0)
        f1 = [sb.tile([P, T], F32, name="f1_0")]
        f2 = sb.tile([P, T], F32, name="f2")
        f3 = sb.tile([P, T], F32, name="f3")
        for win in (f1[0], f2, f3):
            nc.vector.memset(win[:], 0.0)
        for quad in range(PACK):
            nc.vector.tensor_copy(out=c_plane[32 * quad : 32 * quad + PACK, :].bitcast(I32), in_=c_stage[:, quad, :])

        q_dealt = sb.tile([P, PACK, P, PACK], BF16, name="q_dealt", align_bytes=64)
        for h in range(2):
            rows = slice(h * (P // 2), (h + 1) * (P // 2))
            dealt = q_raw[h][:].rearrange("p j (m t) -> p m j t", t=PACK)
            for copy, pair in ((nc.vector.tensor_copy, slice(0, 2)), (nc.scalar.copy, slice(2, 4))):
                copy(out=q_dealt[:, pair, rows, :].rearrange("p t m j -> p m j t"), in_=dealt[:, :, :, pair])
        q_codes = sb.tile([P, Q], U32, name="q_codes", align_bytes=64)
        q_plane = sb.tile([P, Q], U8, name="q_plane", align_bytes=64)
        q_flat = q_dealt[:].rearrange("p t m j -> p (t m j)")
        for c0, c1 in ((0, P), (P, Q)):
            nc.vector.quantize_mx(
                out=q_codes[:, c0:c1].bitcast(FP8X4), scales=q_plane[:, c0:c1], in_=q_flat[:, PACK * c0 : PACK * c1]
            )

        banks = [ps.tile([P, BANK], F32, name="bank%d" % b) for b in range(8)]
        scores = [sb.tile([P, T], F32, name="a%d" % t, tag="a%d" % t) for t in range(PACK - 1)]
        scores.append(placed.tile([P, T], F32, name="a3", offset=0))
        picked = [[sb.tile([P, I], F32, name="pick%d_%d" % (w, t), tag="pick%d_%d" % (w, t)) for w in range(3)] for t in range(PACK)]
        gw = sb.tile([P, I, PACK], BF16, name="gw", align_bytes=64)

        def pieces(t):
            if t == 0:
                return [(banks[b], b * HALF, HALF) for b in range(4)]
            return [(banks[3 - 2 * b], b * BANK, BANK) for b in range(2)]

        def score(t):
            for bank, c, n in pieces(t):
                nc.tensor.matmul_mx(
                    out=bank[:, 0:n],
                    lhsT=q_codes[:, t * P : (t + 1) * P].bitcast(FP8X4),
                    lhsT_scale=q_plane[:, t * P : (t + 1) * P],
                    rhs=c_words[:, c : c + n].bitcast(FP8X4),
                    rhs_scale=c_plane[:, c : c + n],
                    start=True,
                    stop=True,
                )

        def unload(t):
            for b, (bank, c, n) in enumerate(pieces(t)):
                copy = nc.scalar.copy if t == 0 and b % 2 == 0 else nc.vector.tensor_copy
                copy(out=scores[t][:, c : c + n], in_=bank[:, 0:n])

        def cuts(t):
            if t == 0:
                return [(w, c, HALF) for c in (0, HALF) for w in (0, 1)] + [(2, 0, I)]
            return [(w, 0, I) for w in range(3)]

        def look_up(t):
            for w, c, n in cuts(t):
                lst = (idx, idx3, idx5)[w]
                nc.vector.tensor_copy(
                    out=picked[t][w][:, c : c + n], in_=scores[t][:].indirect(lst[:, c // 16 : (c + n) // 16])
                )

        def write(t):
            for w, c, n in cuts(t):
                win, lst = ((f1[t % 2], idx2), (f2, idx4), (f3, idx))[w]
                nc.scalar.activation(win[:].indirect(lst[:, c // 16 : (c + n) // 16]), picked[t][w][:, c : c + n], COPY)

        r = [sb.tile([P, T], F32, name="r%d" % t, tag="a%d" % (t + 1)) for t in range(2)]
        r += [placed.tile([P, T], F32, name="r2", offset=4 * I)] * 2
        g = placed.tile([P, I], F32, name="g", offset=0)

        def larger(t):
            nc.vector.tensor_tensor(r[t][:], f1[t % 2][:], f2[:], ALU.max)

        def less(t):
            nc.vector.tensor_tensor(r[t][:], r[t][:], f3[:], ALU.subtract)

        def read_back(t, n):
            nc.vector.tensor_tensor(g[:, 0:n], r[t][:].indirect(idx6[:, 0 : n // 16]), picked[t][1][:, 0:n], ALU.add)

        def scale(t, c, n):
            nc.vector.tensor_scalar(
                out=gw[:, c : c + n, t], in0=g[:, c : c + n], scalar1=factor[:, t : t + 1], scalar2=None, op0=ALU.mult
            )

        score(0)
        unload(0)
        look_up(0)
        write(0)
        f1.append(sb.tile([P, T], F32, name="f1_1", tag="pick0_0"))
        nc.gpsimd.memset(f1[1][:], 0.0)
        score(1)
        unload(1)
        look_up(1)
        for t in range(2):
            larger(t)
            score(t + 2)
            unload(t + 2)
            less(t)
            write(t + 1)
            look_up(t + 2)
        read_back(0, I)
        larger(2)
        scale(0, 0, I)
        less(2)
        write(3)
        read_back(1, I)
        scale(1, 0, I)
        read_back(2, I)
        larger(3)
        scale(2, 0, I)
        less(3)
        late = sb.tile([P, HALF], F32, name="late")
        nc.scalar.activation(late[:], r[3][:].indirect(idx6[:, HALF // 16 :]), COPY)
        read_back(3, HALF)
        scale(3, 0, HALF)
        nc.vector.tensor_tensor(g[:, HALF:I], late[:], picked[3][1][:, HALF:I], ALU.add)

        g_codes = sb.tile([P, I], U32, name="g_codes", align_bytes=64)
        g_plane = sb.tile([P, I], U8, name="g_plane", align_bytes=64)
        gw_flat = gw[:].rearrange("p i t -> p (i t)")
        out_rows = out.rearrange("(u e) i -> e u i", e=P)
        parts = ((0, HALF), (HALF, P), (HALF + P, P))

        def quantise(c, n):
            nc.vector.quantize_mx(
                out=g_codes[:, c : c + n].bitcast(FP8X4),
                scales=g_plane[:, c : c + n],
                in_=gw_flat[:, PACK * c : PACK * (c + n)],
            )

        quantise(*parts[0])
        scale(PACK - 1, *parts[1])
        scale(PACK - 1, *parts[2])
        quantise(*parts[1])
        quantise(*parts[2])
        for k, (c, n) in enumerate(parts):
            result = sb.tile([P, 2, n], F32, name="result%d" % k)
            for u in range(2):
                bank = banks[2 + 2 * k + u]
                nc.tensor.matmul_mx(
                    out=bank[:, 0:n],
                    lhsT=m_words[:, u * 2 * P : (u + 1) * 2 * P].bitcast(FP4X4),
                    lhsT_scale=m_plane[:, u * P : (u + 1) * P],
                    rhs=g_codes[:, c : c + n].bitcast(FP8X4),
                    rhs_scale=g_plane[:, c : c + n],
                    start=True,
                    stop=True,
                )
                copy = nc.vector.tensor_copy if k == len(parts) - 1 and u == 1 else nc.scalar.copy
                copy(out=result[:, u, :], in_=bank[:, 0:n])
            nc.sync.dma_start(out=out_rows[:, :, c : c + n], in_=result[:])
